import numpy as np
import ml_dtypes


def mxq(x, axis, fmt="e4m3"):
    dtype, down = {"e4m3": (ml_dtypes.float8_e4m3fn, 7), "e5m2": (ml_dtypes.float8_e5m2, 14)}[fmt]
    v = np.moveaxis(np.asarray(x, np.float32).astype(ml_dtypes.bfloat16).astype(np.float64), axis, -1)
    blocks = v.reshape(v.shape[:-1] + (-1, 32))
    amax = np.abs(blocks).max(-1, keepdims=True)
    byte = np.maximum(np.where(amax > 0, np.frexp(amax)[1] - 1 + 127, 0) - down, 1)
    scale = np.exp2(byte - 127.0)
    codes = (blocks / scale).astype(np.float32).astype(dtype).astype(np.float64)
    return np.moveaxis((codes * scale).reshape(v.shape), -1, axis)


WIDE = False


def mx_kscale(k):
    if not WIDE:
        return np.ones(k)
    levels = np.array([10, -10, 5, -5, 0])
    if k % 512:
        return np.exp2(np.random.permutation(np.resize(levels, k // 32))).repeat(32)
    a = np.empty((k // 512, 16))
    for p in range(k // 512):
        a[p, :8] = np.random.permutation(np.resize(levels, 8))
        for g in range(8):
            far = levels[np.abs(levels - a[p, g]) >= 10]
            a[p, g + 8] = far[np.random.randint(len(far))]
    return np.exp2(a.ravel()).repeat(32)


def f64(x):
    return np.asarray(x).astype(np.float64)


def striped(idx):
    return np.tile(idx.reshape(-1, 16).T, (8, 1)).astype(np.uint16)


def unstriped(offs):
    return offs[:16].T.reshape(-1).astype(np.int64)


def striped8(idx):
    return np.concatenate([x.reshape(-1, 16).T for x in idx]).astype(np.uint16)


def runs(offs, k):
    lists = np.stack([offs[16 * r : 16 * r + 16].T.reshape(-1) for r in range(8)]).astype(np.int64)
    return lists[np.arange(k) % 512 // 64]


def pack_weight(w):
    k, n = w.shape
    w = f64(np.asarray(w, np.float32).astype(ml_dtypes.bfloat16)).reshape(k // 32, 32, n)
    amax = np.abs(w).max(1)
    byte = np.clip(np.where(amax > 0, np.frexp(amax)[1] - 1 + 127 - 7, 1), 1, 254)
    scaled = (w * np.exp2(127.0 - byte)[:, None, :]).reshape(k, n).astype(np.float32)
    words = np.ascontiguousarray(scaled.reshape(k // 512, 128, 4, n).transpose(0, 1, 3, 2)).astype(ml_dtypes.float8_e4m3fn).view(np.uint8)
    return words, np.ascontiguousarray(byte.astype(np.uint8).reshape(k // 512, 16, n))


def unpack_weight(words, scales):
    g, p, n, _ = words.shape
    vals = np.ascontiguousarray(words).view(ml_dtypes.float8_e4m3fn).astype(np.float64) * np.repeat(np.exp2(scales.astype(np.float64) - 127.0), 8, axis=1)[..., None]
    return vals.transpose(0, 1, 3, 2).reshape(g * 512, n)


def relu(v):
    return np.maximum(v, 0.0)


K, T, S, N, H = 512, 2048, 512, 512, 512


def setup_inputs():
    n = np.random.standard_normal
    s = mx_kscale(K)[:, None]
    u = mx_kscale(S)
    packed_xT = pack_weight(n((K, T)) * s)
    return {
        "x_words": packed_xT[0],
        "x_scales": packed_xT[1],
        "wa": (n((K, H)) / np.sqrt(K) / s).astype(np.float32),
        "gt": (np.random.uniform(0.5, 1.5, (S, 1)) * u[:, None]).astype(np.float32),
        "w1": (n((S, H)) / np.sqrt(S) / u[:, None]).astype(np.float32),
        "gp": (np.random.uniform(0.5, 1.5, (H, 1)) * u[:, None]).astype(np.float32),
        "res": (1.5 * n((N, H))).astype(np.float32),
        "w2": (n((H, N)) / np.sqrt(H) / u[:, None]).astype(np.float32),
        "offs": striped(np.random.permutation(T)[:S]),
        "fl": striped8(np.stack([np.random.permutation(H) for _ in range(8)])),
        "fm": striped8(np.stack([np.random.permutation(H) for _ in range(8)])),
    }


def reference(x_words, x_scales, wa, gt, w1, gp, res, w2, offs, fl, fm):
    xq = unpack_weight(x_words, x_scales)[:, unstriped(offs)]
    y = xq.T @ mxq(f64(wa), 0, "e4m3")
    z = f64(gt) * (y[np.arange(S)[:, None], runs(fl, S)])
    h = relu(mxq(f64(w1), 0, "e4m3").T @ mxq(z, 0, "e4m3"))
    z2 = f64(gp) * (h[np.arange(H)[:, None], runs(fm, H)])
    return f64(res) + (mxq(f64(w2), 0, "e4m3").T @ mxq(z2, 0, "e4m3"))

@@ -1,0 +1,172 @@
+from contextlib import ExitStack
+
+import concourse.mybir as mybir
+
+K, T, S, H, N = 512, 2048, 512, 512, 512
+FLOPS = 3 * 2 * 512 * 512 * 512
+
+F32 = mybir.dt.float32
+BF16 = mybir.dt.bfloat16
+I32 = mybir.dt.int32
+U32 = mybir.dt.uint32
+U16 = mybir.dt.uint16
+U8 = mybir.dt.uint8
+FP8X4 = mybir.dt.float8_e4m3fn_x4
+ACT = mybir.ActivationFunctionType
+ALU = mybir.AluOpType
+
+P = 128
+PACK = 4
+LIST_ROWS = 16
+WA_CHUNKS = ((0, 256), (256, 256))
+Z_CHUNKS = ((0, 256), (256, 256))
+Z2_CHUNKS = ((0, 256), (256, 128), (384, 128))
+
+
+def tile_picked_mixdeep_relu_p_kernel(
+    tc, x_words, x_scales, wa, gt, w1, gp, res, w2, offs, fl, fm, out
+):
+    nc = tc.nc
+    with ExitStack() as ctx:
+        keep = ctx.enter_context(tc.tile_pool(name="keep", bufs=1))
+        psum = ctx.enter_context(tc.psum_pool(name="psum", bufs=1))
+
+        def sb(name, shape, dtype):
+            return keep.tile(shape, dtype, name=name, align_bytes=64)
+
+        def interleave(engine, grouped, planes):
+            dst = grouped.rearrange("p (c i t) -> p c t i", i=4, t=PACK)
+            src = planes.rearrange("p t (c i) -> p c t i", i=4)
+            if engine == "vector":
+                nc.vector.tensor_copy(dst, src)
+            else:
+                nc.scalar.activation(dst, src, ACT.Copy)
+
+        def quantize(codes, scales, grouped):
+            nc.vector.quantize_mx(out=codes.bitcast(FP8X4), scales=scales, in_=grouped)
+
+        def matmul(acc, lhs_codes, lhs_scales, rhs_codes, rhs_scales):
+            nc.tensor.matmul_mx(
+                out=acc, lhsT=lhs_codes.bitcast(FP8X4), lhsT_scale=lhs_scales,
+                rhs=rhs_codes.bitcast(FP8X4), rhs_scale=rhs_scales, start=True, stop=True,
+            )
+
+        offs_sb = keep.tile([P, S // LIST_ROWS], U16, name="offs_sb")
+        fl_sb = keep.tile([P, H // LIST_ROWS], U16, name="fl_sb")
+        fm_sb = keep.tile([P, H // LIST_ROWS], U16, name="fm_sb")
+        x_words_sb = sb("x_words_sb", [P, T], U32)
+        x_scales_sb = sb("x_scales_sb", [P, T], U8)
+        gt_sb = sb("gt_sb", [P, PACK], F32)
+        gp_sb = sb("gp_sb", [P, PACK], F32)
+        wa_raw = [sb("wa_raw%d" % c0, [P, PACK, n], F32) for c0, n in WA_CHUNKS]
+        w1_raw = sb("w1_raw", [P, PACK, H], F32)
+        w2_raw = sb("w2_raw", [P, PACK, N], F32)
+        res_sb = sb("res_sb", [P, PACK, H], F32)
+
+        nc.vector.memset(x_scales_sb[:].bitcast(I32), 0)
+        nc.sync.dma_start(x_words_sb[:].bitcast(I32), x_words[0].rearrange("p n t -> p (n t)").bitcast(I32))
+        for q in range(4):
+            nc.sync.dma_start(
+                x_scales_sb[32 * q : 32 * q + 4, :].bitcast(I32), x_scales[0, 4 * q : 4 * q + 4, :].bitcast(I32)
+            )
+        nc.sync.dma_start(offs_sb[:], offs)
+        wa_rows = wa.rearrange("(p j) c -> p j c", j=PACK)
+        for (c0, n), raw in zip(WA_CHUNKS, wa_raw):
+            nc.sync.dma_start(raw[:], wa_rows[:, :, c0 : c0 + n])
+        nc.sync.dma_start(gt_sb[:], gt.rearrange("(p t) o -> p (t o)", t=PACK))
+        nc.sync.dma_start(fl_sb[:], fl)
+        nc.sync.dma_start(w1_raw[:], w1.rearrange("(p j) c -> p j c", j=PACK))
+        nc.sync.dma_start(gp_sb[:], gp.rearrange("(p t) o -> p (t o)", t=PACK))
+        nc.sync.dma_start(fm_sb[:], fm)
+        nc.sync.dma_start(w2_raw[:], w2.rearrange("(p j) c -> p j c", j=PACK))
+        nc.sync.dma_start(res_sb[:], res.rearrange("(t p) c -> p t c", p=P))
+
+        picked_scales = sb("picked_scales", [P, S], U8)
+        x_codes = sb("x_codes", [P, S], U32)
+        x_plane = sb("x_plane", [P, S], U8)
+        nc.vector.tensor_copy(picked_scales[:], x_scales_sb[:].indirect(offs_sb[:]))
+        nc.vector.tensor_copy(
+            x_plane[:].rearrange("p (t m) -> p t m", t=PACK), picked_scales[:].rearrange("p (m t) -> p t m", t=PACK)
+        )
+        nc.vector.tensor_copy(x_codes[:].rearrange("p (t m) -> p m t", t=PACK), x_words_sb[:].indirect(offs_sb[:]))
+
+        wa_grouped = [sb("wa_grouped%d" % c0, [P, PACK * n], BF16) for c0, n in WA_CHUNKS]
+        wa_codes = [sb("wa_codes%d" % c0, [P, n], U32) for c0, n in WA_CHUNKS]
+        wa_plane = [sb("wa_plane%d" % c0, [P, n], U8) for c0, n in WA_CHUNKS]
+        interleave("scalar", wa_grouped[0][:], wa_raw[0][:])
+        quantize(wa_codes[0][:], wa_plane[0][:], wa_grouped[0][:])
+        interleave("scalar", wa_grouped[1][:, 0:512], wa_raw[1][:, :, 0:128])
+        interleave("vector", wa_grouped[1][:, 512:1024], wa_raw[1][:, :, 128:256])
+        quantize(wa_codes[1][:], wa_plane[1][:], wa_grouped[1][:])
+
+        y_acc = [psum.tile([P, H], F32, name="y_acc%d" % t, tag="outer%d" % t) for t in range(PACK)]
+        y_sb = [sb("y_sb%d" % t, [P, H], F32) for t in range(PACK)]
+        for c, (c0, n) in enumerate(WA_CHUNKS):
+            for t in range(PACK):
+                rows = slice(t * P, (t + 1) * P)
+                matmul(y_acc[t][:, c0 : c0 + n], x_codes[:, rows], x_plane[:, rows], wa_codes[c][:], wa_plane[c][:])
+        for t in range(PACK):
+            nc.scalar.activation(y_sb[t][:], y_acc[t][:], ACT.Copy, scale=gt_sb[:, t : t + 1])
+
+        w1_grouped = sb("w1_grouped", [P, PACK * H], BF16)
+        w1_codes = sb("w1_codes", [P, H], U32)
+        w1_plane = sb("w1_plane", [P, H], U8)
+
+        def fetch(name, windows, lists, c0, n):
+            planes = sb("%s_planes%d" % (name, c0), [P, PACK, n], BF16)
+            for t in range(PACK):
+                picks = lists[:, c0 // LIST_ROWS : (c0 + n) // LIST_ROWS]
+                nc.vector.tensor_copy(planes[:, t, :], windows[t][:].indirect(picks))
+            return planes
+
+        def pack(name, engine, planes, c0, n):
+            grouped = sb("%s_grouped%d" % (name, c0), [P, PACK * n], BF16)
+            codes = sb("%s_codes%d" % (name, c0), [P, n], U32)
+            plane = sb("%s_plane%d" % (name, c0), [P, n], U8)
+            interleave(engine, grouped[:], planes[:])
+            quantize(codes[:], plane[:], grouped[:])
+            return codes, plane
+
+        z_planes = [fetch("z", y_sb, fl_sb, c0, n) for c0, n in Z_CHUNKS]
+        nc.scalar.activation(
+            w1_grouped[:].rearrange("p (t m j) -> p m j t", t=PACK, j=PACK),
+            w1_raw[:].rearrange("p j (m t) -> p m j t", t=PACK),
+            ACT.Copy,
+        )
+        quantize(w1_codes[:], w1_plane[:], w1_grouped[:])
+
+        h_sb = [sb("h_sb%d" % t, [P, H], F32) for t in range(PACK)]
+        for c, (c0, n) in enumerate(Z_CHUNKS):
+            codes, plane = pack("z", "scalar" if c == 0 else "vector", z_planes[c], c0, n)
+            h_acc = [psum.tile([P, 2, n], F32, name="h_acc%d_%d" % (c, u), tag="inner%d" % (2 * c + u)) for u in range(2)]
+            for t in range(PACK):
+                rows = slice(t * P, (t + 1) * P)
+                matmul(h_acc[t // 2][:, t % 2, :], w1_codes[:, rows], w1_plane[:, rows], codes[:], plane[:])
+            for t in range(PACK):
+                nc.vector.tensor_scalar(
+                    h_sb[t][:, c0 : c0 + n], h_acc[t // 2][:, t % 2, :], 0.0, gp_sb[:, t : t + 1], ALU.max, ALU.mult
+                )
+
+        w2_grouped = sb("w2_grouped", [P, PACK * N], BF16)
+        w2_codes = sb("w2_codes", [P, N], U32)
+        w2_plane = sb("w2_plane", [P, N], U8)
+        interleave("scalar", w2_grouped[:], w2_raw[:])
+        quantize(w2_codes[:], w2_plane[:], w2_grouped[:])
+
+        out_rows = out.rearrange("(t p) c -> p t c", p=P)
+        z2_planes = [fetch("z2", h_sb, fm_sb, c0, n) for c0, n in Z2_CHUNKS]
+        bank = 0
+        for c, (c0, n) in enumerate(Z2_CHUNKS):
+            last = c == len(Z2_CHUNKS) - 1
+            codes, plane = pack("z2", "vector" if last else "scalar", z2_planes[c], c0, n)
+            per_bank = 512 // n
+            result = sb("result%d" % c0, [P, PACK, n], F32)
+            for t0 in range(0, PACK, per_bank):
+                acc = psum.tile([P, per_bank, n], F32, name="out_acc%d" % bank, tag="outer%d" % bank)
+                bank = bank + 1
+                for t in range(t0, t0 + per_bank):
+                    rows = slice(t * P, (t + 1) * P)
+                    matmul(acc[:, t - t0, :], w2_codes[:, rows], w2_plane[:, rows], codes[:], plane[:])
+                tiles = slice(t0, t0 + per_bank)
+                nc.vector.tensor_tensor(result[:, tiles, :], acc[:], res_sb[:, tiles, c0 : c0 + n], ALU.add)
+            nc.sync.dma_start(out_rows[:, :, c0 : c0 + n], result[:])

@@ -18,9 +18,8 @@ ALU = mybir.AluOpType
 P = 128
 PACK = 4
 LIST_ROWS = 16
-WA_CHUNKS = ((0, 256), (256, 256))
-Z_CHUNKS = ((0, 256), (256, 256))
-Z2_CHUNKS = ((0, 256), (256, 128), (384, 128))
+HALF = 256
+WA_SCALAR_COLUMNS = 96
 
 
 def tile_picked_mixdeep_relu_p_kernel(
@@ -31,24 +30,29 @@ def tile_picked_mixdeep_relu_p_kernel(
         keep = ctx.enter_context(tc.tile_pool(name="keep", bufs=1))
         psum = ctx.enter_context(tc.psum_pool(name="psum", bufs=1))
 
-        def sb(name, shape, dtype):
-            return keep.tile(shape, dtype, name=name, align_bytes=64)
+        def sb(name, shape, dtype, tag=None):
+            return keep.tile(shape, dtype, name=name, tag=tag or name, align_bytes=64)
 
-        def interleave(engine, grouped, planes):
-            dst = grouped.rearrange("p (c i t) -> p c t i", i=4, t=PACK)
-            src = planes.rearrange("p t (c i) -> p c t i", i=4)
-            if engine == "vector":
-                nc.vector.tensor_copy(dst, src)
-            else:
-                nc.scalar.activation(dst, src, ACT.Copy)
+        def bank(name, shape, number):
+            return psum.tile(shape, F32, name=name, tag="bank%d" % number)
 
-        def quantize(codes, scales, grouped):
-            nc.vector.quantize_mx(out=codes.bitcast(FP8X4), scales=scales, in_=grouped)
+        def half(c):
+            return slice(c * HALF, (c + 1) * HALF)
 
-        def matmul(acc, lhs_codes, lhs_scales, rhs_codes, rhs_scales):
+        def interleave(copy, grouped, planes):
+            copy(grouped.rearrange("p (c i t) -> p c t i", i=4, t=PACK), planes.rearrange("p t (c i) -> p c t i", i=4))
+
+        def quantize(name, grouped):
+            codes = sb(name + "_codes", [P, HALF], U32)
+            scales = sb(name + "_scales", [P, HALF], U8)
+            nc.vector.quantize_mx(out=codes[:].bitcast(FP8X4), scales=scales[:], in_=grouped[:])
+            return codes, scales
+
+        def matmul(acc, stationary, tile_in_pair, moving):
+            rows = slice(tile_in_pair * P, (tile_in_pair + 1) * P)
             nc.tensor.matmul_mx(
-                out=acc, lhsT=lhs_codes.bitcast(FP8X4), lhsT_scale=lhs_scales,
-                rhs=rhs_codes.bitcast(FP8X4), rhs_scale=rhs_scales, start=True, stop=True,
+                out=acc, lhsT=stationary[0][:, rows].bitcast(FP8X4), lhsT_scale=stationary[1][:, rows],
+                rhs=moving[0].bitcast(FP8X4), rhs_scale=moving[1], start=True, stop=True,
             )
 
         offs_sb = keep.tile([P, S // LIST_ROWS], U16, name="offs_sb")
@@ -56,29 +60,32 @@ def tile_picked_mixdeep_relu_p_kernel(
         fm_sb = keep.tile([P, H // LIST_ROWS], U16, name="fm_sb")
         x_words_sb = sb("x_words_sb", [P, T], U32)
         x_scales_sb = sb("x_scales_sb", [P, T], U8)
-        gt_sb = sb("gt_sb", [P, PACK], F32)
-        gp_sb = sb("gp_sb", [P, PACK], F32)
-        wa_raw = [sb("wa_raw%d" % c0, [P, PACK, n], F32) for c0, n in WA_CHUNKS]
+        gt_sb = sb("gt_sb", [P, PACK], F32, "z_late")
+        z2_planes = [sb("z2_planes%d" % c, [P, PACK * HALF], BF16, ("z2_early", "z2_late")[c]) for c in range(2)]
+        gp_sb = z2_planes[1][:, 2 * HALF : 2 * HALF + 2 * PACK].bitcast(F32)
+        wa_raw = [sb("wa_raw%d" % c, [P, PACK, HALF], F32) for c in range(2)]
         w1_raw = sb("w1_raw", [P, PACK, H], F32)
-        w2_raw = sb("w2_raw", [P, PACK, N], F32)
+        w2_raw = [sb("w2_raw%d" % c, [P, PACK, HALF], F32) for c in range(2)]
         res_sb = sb("res_sb", [P, PACK, H], F32)
 
-        nc.vector.memset(x_scales_sb[:].bitcast(I32), 0)
-        nc.sync.dma_start(x_words_sb[:].bitcast(I32), x_words[0].rearrange("p n t -> p (n t)").bitcast(I32))
+        wa_rows = wa.rearrange("(p j) c -> p j c", j=PACK)
+        w2_rows = w2.rearrange("(p j) c -> p j c", j=PACK)
+        nc.gpsimd.memset(x_scales_sb[:].bitcast(I32), 0)
+        nc.scalar.dma_start(gt_sb[:], gt.rearrange("(p t) o -> p (t o)", t=PACK))
+        nc.sync.dma_start(wa_raw[0][:], wa_rows[:, :, half(0)])
         for q in range(4):
             nc.sync.dma_start(
                 x_scales_sb[32 * q : 32 * q + 4, :].bitcast(I32), x_scales[0, 4 * q : 4 * q + 4, :].bitcast(I32)
             )
         nc.sync.dma_start(offs_sb[:], offs)
-        wa_rows = wa.rearrange("(p j) c -> p j c", j=PACK)
-        for (c0, n), raw in zip(WA_CHUNKS, wa_raw):
-            nc.sync.dma_start(raw[:], wa_rows[:, :, c0 : c0 + n])
-        nc.sync.dma_start(gt_sb[:], gt.rearrange("(p t) o -> p (t o)", t=PACK))
+        nc.sync.dma_start(x_words_sb[:].bitcast(I32), x_words[0].rearrange("p n t -> p (n t)").bitcast(I32))
+        nc.sync.dma_start(wa_raw[1][:], wa_rows[:, :, half(1)])
         nc.sync.dma_start(fl_sb[:], fl)
         nc.sync.dma_start(w1_raw[:], w1.rearrange("(p j) c -> p j c", j=PACK))
-        nc.sync.dma_start(gp_sb[:], gp.rearrange("(p t) o -> p (t o)", t=PACK))
+        nc.sync.dma_start(w2_raw[0][:], w2_rows[:, :, half(0)])
+        nc.sync.dma_start(gp_sb, gp.rearrange("(p t) o -> p (t o)", t=PACK))
         nc.sync.dma_start(fm_sb[:], fm)
-        nc.sync.dma_start(w2_raw[:], w2.rearrange("(p j) c -> p j c", j=PACK))
+        nc.sync.dma_start(w2_raw[1][:], w2_rows[:, :, half(1)])
         nc.sync.dma_start(res_sb[:], res.rearrange("(t p) c -> p t c", p=P))
 
         picked_scales = sb("picked_scales", [P, S], U8)
@@ -89,84 +96,100 @@ def tile_picked_mixdeep_relu_p_kernel(
             x_plane[:].rearrange("p (t m) -> p t m", t=PACK), picked_scales[:].rearrange("p (m t) -> p t m", t=PACK)
         )
         nc.vector.tensor_copy(x_codes[:].rearrange("p (t m) -> p m t", t=PACK), x_words_sb[:].indirect(offs_sb[:]))
+        x_packed = (x_codes, x_plane)
 
-        wa_grouped = [sb("wa_grouped%d" % c0, [P, PACK * n], BF16) for c0, n in WA_CHUNKS]
-        wa_codes = [sb("wa_codes%d" % c0, [P, n], U32) for c0, n in WA_CHUNKS]
-        wa_plane = [sb("wa_plane%d" % c0, [P, n], U8) for c0, n in WA_CHUNKS]
-        interleave("scalar", wa_grouped[0][:], wa_raw[0][:])
-        quantize(wa_codes[0][:], wa_plane[0][:], wa_grouped[0][:])
-        interleave("scalar", wa_grouped[1][:, 0:512], wa_raw[1][:, :, 0:128])
-        interleave("vector", wa_grouped[1][:, 512:1024], wa_raw[1][:, :, 128:256])
-        quantize(wa_codes[1][:], wa_plane[1][:], wa_grouped[1][:])
+        wa_grouped = [sb("wa_grouped%d" % c, [P, PACK * HALF], BF16) for c in range(2)]
+        wa_codes = sb("wa_codes", [P, H], U32)
+        wa_plane = sb("wa_plane", [P, H], U8, "picked_scales")
+        cut = WA_SCALAR_COLUMNS
+        interleave(nc.scalar.copy, wa_grouped[0][:], wa_raw[0][:])
+        interleave(nc.scalar.copy, wa_grouped[1][:, 0 : PACK * cut], wa_raw[1][:, :, 0:cut])
+        interleave(nc.vector.tensor_copy, wa_grouped[1][:, PACK * cut : PACK * HALF], wa_raw[1][:, :, cut:HALF])
+        for c in range(2):
+            nc.vector.quantize_mx(
+                out=wa_codes[:, half(c)].bitcast(FP8X4), scales=wa_plane[:, half(c)], in_=wa_grouped[c][:]
+            )
 
-        y_acc = [psum.tile([P, H], F32, name="y_acc%d" % t, tag="outer%d" % t) for t in range(PACK)]
-        y_sb = [sb("y_sb%d" % t, [P, H], F32) for t in range(PACK)]
-        for c, (c0, n) in enumerate(WA_CHUNKS):
-            for t in range(PACK):
-                rows = slice(t * P, (t + 1) * P)
-                matmul(y_acc[t][:, c0 : c0 + n], x_codes[:, rows], x_plane[:, rows], wa_codes[c][:], wa_plane[c][:])
-        for t in range(PACK):
-            nc.scalar.activation(y_sb[t][:], y_acc[t][:], ACT.Copy, scale=gt_sb[:, t : t + 1])
+        y_rows = [sb("y_rows%d" % t, [P, H], F32, "wa_raw1" if t == 0 else None) for t in range(PACK)]
+        for c in range(2):
+            acc = bank("y_first%d" % c, [P, HALF], (4, 0)[c])
+            matmul(acc[:], x_packed, 0, (wa_codes[:, half(c)], wa_plane[:, half(c)]))
+            nc.scalar.activation(y_rows[0][:, half(c)], acc[:], ACT.Copy, scale=gt_sb[:, 0:1])
+        for t in range(1, PACK):
+            acc = bank("y_acc%d" % t, [P, H], t)
+            matmul(acc[:], x_packed, t, (wa_codes[:], wa_plane[:]))
+            nc.scalar.activation(y_rows[t][:], acc[:], ACT.Copy, scale=gt_sb[:, t : t + 1])
 
-        w1_grouped = sb("w1_grouped", [P, PACK * H], BF16)
-        w1_codes = sb("w1_codes", [P, H], U32)
-        w1_plane = sb("w1_plane", [P, H], U8)
+        def fetch(planes, rows, lists, order):
+            for t, c in order:
+                picks = lists[:, c * HALF // LIST_ROWS : (c + 1) * HALF // LIST_ROWS]
+                nc.vector.tensor_copy(planes[c][:, t * HALF : (t + 1) * HALF], rows[t][:].indirect(picks))
 
-        def fetch(name, windows, lists, c0, n):
-            planes = sb("%s_planes%d" % (name, c0), [P, PACK, n], BF16)
-            for t in range(PACK):
-                picks = lists[:, c0 // LIST_ROWS : (c0 + n) // LIST_ROWS]
-                nc.vector.tensor_copy(planes[:, t, :], windows[t][:].indirect(picks))
-            return planes
+        def weave(name, copy, planes, tag=None):
+            grouped = sb(name, [P, PACK * HALF], BF16, tag)
+            interleave(copy, grouped[:], planes[:].rearrange("p (t c) -> p t c", t=PACK))
+            return grouped
 
-        def pack(name, engine, planes, c0, n):
-            grouped = sb("%s_grouped%d" % (name, c0), [P, PACK * n], BF16)
-            codes = sb("%s_codes%d" % (name, c0), [P, n], U32)
-            plane = sb("%s_plane%d" % (name, c0), [P, n], U8)
-            interleave(engine, grouped[:], planes[:])
-            quantize(codes[:], plane[:], grouped[:])
-            return codes, plane
+        def deal_w1(pair):
+            grouped = sb("w1_grouped%d" % pair, [P, PACK * HALF], BF16)
+            nc.scalar.copy(
+                grouped[:].rearrange("p (t m j) -> p m j t", t=2, j=PACK),
+                w1_raw[:].rearrange("p j (m t) -> p m j t", t=PACK)[:, :, :, 2 * pair : 2 * pair + 2],
+            )
+            return grouped
 
-        z_planes = [fetch("z", y_sb, fl_sb, c0, n) for c0, n in Z_CHUNKS]
-        nc.scalar.activation(
-            w1_grouped[:].rearrange("p (t m j) -> p m j t", t=PACK, j=PACK),
-            w1_raw[:].rearrange("p j (m t) -> p m j t", t=PACK),
-            ACT.Copy,
-        )
-        quantize(w1_codes[:], w1_plane[:], w1_grouped[:])
+        def cast_w2(c, tag=None):
+            grouped = sb("w2_grouped%d" % c, [P, PACK * HALF], BF16, tag)
+            interleave(nc.scalar.copy, grouped[:], w2_raw[c][:])
+            return grouped
 
-        h_sb = [sb("h_sb%d" % t, [P, H], F32) for t in range(PACK)]
-        for c, (c0, n) in enumerate(Z_CHUNKS):
-            codes, plane = pack("z", "scalar" if c == 0 else "vector", z_planes[c], c0, n)
-            h_acc = [psum.tile([P, 2, n], F32, name="h_acc%d_%d" % (c, u), tag="inner%d" % (2 * c + u)) for u in range(2)]
-            for t in range(PACK):
-                rows = slice(t * P, (t + 1) * P)
-                matmul(h_acc[t // 2][:, t % 2, :], w1_codes[:, rows], w1_plane[:, rows], codes[:], plane[:])
-            for t in range(PACK):
-                nc.vector.tensor_scalar(
-                    h_sb[t][:, c0 : c0 + n], h_acc[t // 2][:, t % 2, :], 0.0, gp_sb[:, t : t + 1], ALU.max, ALU.mult
-                )
+        z_planes = [sb("z_planes%d" % c, [P, PACK * HALF], BF16, ("z_early", "z_late")[c]) for c in range(2)]
+        fetch(z_planes, y_rows, fl_sb, [(t, c) for c in range(2) for t in range(PACK)])
+        w1_packed = [quantize("w1_first", deal_w1(0))]
+        z_packed = [quantize("z_first", weave("z_grouped0", nc.scalar.copy, z_planes[0]))]
+        z_grouped = weave("z_grouped1", nc.vector.tensor_copy, z_planes[1], "z_early")
+        w1_packed.append(quantize("w1_second", deal_w1(1)))
+        z_packed.append(quantize("z_second", z_grouped))
+        w2_grouped = cast_w2(0)
 
-        w2_grouped = sb("w2_grouped", [P, PACK * N], BF16)
-        w2_codes = sb("w2_codes", [P, N], U32)
-        w2_plane = sb("w2_plane", [P, N], U8)
-        interleave("scalar", w2_grouped[:], w2_raw[:])
-        quantize(w2_codes[:], w2_plane[:], w2_grouped[:])
+        h_rows = [sb("h_rows0", [P, H], F32, "z_late")] + y_rows[1:]
+        h_relu = sb("h_relu", [P, 5 * HALF], F32, "w2_raw0")
+
+        def h_product(acc, t, c):
+            matmul(acc, w1_packed[t // 2], t % 2, (z_packed[c][0][:], z_packed[c][1][:]))
+
+        def h_on_vector(t, c, number):
+            acc = bank("h_acc%d_%d" % (t, c), [P, HALF], number)
+            h_product(acc[:], t, c)
+            nc.vector.tensor_scalar(h_rows[t][:, half(c)], acc[:], 0.0, gp_sb[:, t : t + 1], ALU.max, ALU.mult)
+
+        def h_on_scalar(t, halves, number, staged):
+            acc = bank("h_acc%d" % t, [P, len(halves) * HALF], number)
+            for c in halves:
+                h_product(acc[:, half(c)], t, c)
+            nc.scalar.activation(staged, acc[:], ACT.Relu)
+            nc.scalar.activation(h_rows[t][:, 0 : len(halves) * HALF], staged, ACT.Copy, scale=gp_sb[:, t : t + 1])
+
+        h_on_vector(0, 0, 4)
+        w2_packed = [quantize("w2_first", w2_grouped)]
+        h_on_scalar(1, (0,), 5, h_relu[:, 0:HALF])
+        h_on_vector(0, 1, 0)
+        h_on_vector(1, 1, 1)
+        h_on_scalar(2, (0, 1), 2, h_relu[:, HALF : 3 * HALF])
+        h_on_scalar(3, (0, 1), 4, h_relu[:, 3 * HALF : 5 * HALF])
+
+        fetch(z2_planes, h_rows, fm_sb, [(t, c) for pair in ((0, 1), (2, 3)) for c in range(2) for t in pair])
+        w2_packed.append(quantize("w2_second", cast_w2(1, "w2_raw0")))
+        z2_packed = [quantize("z2_first", weave("z2_grouped0", nc.scalar.copy, z2_planes[0]))]
+        z2_packed.append(quantize("z2_second", weave("z2_grouped1", nc.vector.tensor_copy, z2_planes[1], "z2_early")))
 
         out_rows = out.rearrange("(t p) c -> p t c", p=P)
-        z2_planes = [fetch("z2", h_sb, fm_sb, c0, n) for c0, n in Z2_CHUNKS]
-        bank = 0
-        for c, (c0, n) in enumerate(Z2_CHUNKS):
-            last = c == len(Z2_CHUNKS) - 1
-            codes, plane = pack("z2", "vector" if last else "scalar", z2_planes[c], c0, n)
-            per_bank = 512 // n
-            result = sb("result%d" % c0, [P, PACK, n], F32)
-            for t0 in range(0, PACK, per_bank):
-                acc = psum.tile([P, per_bank, n], F32, name="out_acc%d" % bank, tag="outer%d" % bank)
-                bank = bank + 1
-                for t in range(t0, t0 + per_bank):
-                    rows = slice(t * P, (t + 1) * P)
-                    matmul(acc[:, t - t0, :], w2_codes[:, rows], w2_plane[:, rows], codes[:], plane[:])
-                tiles = slice(t0, t0 + per_bank)
-                nc.vector.tensor_tensor(result[:, tiles, :], acc[:], res_sb[:, tiles, c0 : c0 + n], ALU.add)
-            nc.sync.dma_start(out_rows[:, :, c0 : c0 + n], result[:])
+        groups = (((0, 2, 6), (2, 4, 7)), ((0, 2, 0), (2, 3, 1), (3, 4, 3)))
+        for c in range(2):
+            result = sb("result%d" % c, [P, PACK, HALF], F32, ("z2_late", None)[c])
+            for first, last, number in groups[c]:
+                acc = bank("out_acc%d_%d" % (c, first), [P, last - first, HALF], number)
+                for t in range(first, last):
+                    matmul(acc[:, t - first, :], w2_packed[t // 2], t % 2, (z2_packed[c][0][:], z2_packed[c][1][:]))
+                nc.vector.tensor_tensor(result[:, first:last, :], acc[:], res_sb[:, first:last, half(c)], ALU.add)
+                nc.sync.dma_start(out_rows[:, first:last, half(c)], result[:, first:last, :])

from contextlib import ExitStack

import concourse.mybir as mybir

K, T, S, H, N = 512, 2048, 512, 512, 512
FLOPS = 3 * 2 * 512 * 512 * 512

F32 = mybir.dt.float32
BF16 = mybir.dt.bfloat16
I32 = mybir.dt.int32
U32 = mybir.dt.uint32
U16 = mybir.dt.uint16
U8 = mybir.dt.uint8
FP8X4 = mybir.dt.float8_e4m3fn_x4
ACT = mybir.ActivationFunctionType
ALU = mybir.AluOpType

P = 128
PACK = 4
LIST_ROWS = 16
HALF = 256
WA_SCALAR_COLUMNS = 96


def tile_picked_mixdeep_relu_p_kernel(
    tc, x_words, x_scales, wa, gt, w1, gp, res, w2, offs, fl, fm, out
):
    nc = tc.nc
    with ExitStack() as ctx:
        keep = ctx.enter_context(tc.tile_pool(name="keep", bufs=1))
        psum = ctx.enter_context(tc.psum_pool(name="psum", bufs=1))

        def sb(name, shape, dtype, tag=None):
            return keep.tile(shape, dtype, name=name, tag=tag or name, align_bytes=64)

        def bank(name, shape, number):
            return psum.tile(shape, F32, name=name, tag="bank%d" % number)

        def half(c):
            return slice(c * HALF, (c + 1) * HALF)

        def interleave(copy, grouped, planes):
            copy(grouped.rearrange("p (c i t) -> p c t i", i=4, t=PACK), planes.rearrange("p t (c i) -> p c t i", i=4))

        def quantize(name, grouped):
            codes = sb(name + "_codes", [P, HALF], U32)
            scales = sb(name + "_scales", [P, HALF], U8)
            nc.vector.quantize_mx(out=codes[:].bitcast(FP8X4), scales=scales[:], in_=grouped[:])
            return codes, scales

        def matmul(acc, stationary, tile_in_pair, moving):
            rows = slice(tile_in_pair * P, (tile_in_pair + 1) * P)
            nc.tensor.matmul_mx(
                out=acc, lhsT=stationary[0][:, rows].bitcast(FP8X4), lhsT_scale=stationary[1][:, rows],
                rhs=moving[0].bitcast(FP8X4), rhs_scale=moving[1], start=True, stop=True,
            )

        offs_sb = keep.tile([P, S // LIST_ROWS], U16, name="offs_sb")
        fl_sb = keep.tile([P, H // LIST_ROWS], U16, name="fl_sb")
        fm_sb = keep.tile([P, H // LIST_ROWS], U16, name="fm_sb")
        x_words_sb = sb("x_words_sb", [P, T], U32)
        x_scales_sb = sb("x_scales_sb", [P, T], U8)
        gt_sb = sb("gt_sb", [P, PACK], F32, "z_late")
        z2_planes = [sb("z2_planes%d" % c, [P, PACK * HALF], BF16, ("z2_early", "z2_late")[c]) for c in range(2)]
        gp_sb = z2_planes[1][:, 2 * HALF : 2 * HALF + 2 * PACK].bitcast(F32)
        wa_raw = [sb("wa_raw%d" % c, [P, PACK, HALF], F32) for c in range(2)]
        w1_raw = sb("w1_raw", [P, PACK, H], F32)
        w2_raw = [sb("w2_raw%d" % c, [P, PACK, HALF], F32) for c in range(2)]
        res_sb = sb("res_sb", [P, PACK, H], F32)

        wa_rows = wa.rearrange("(p j) c -> p j c", j=PACK)
        w2_rows = w2.rearrange("(p j) c -> p j c", j=PACK)
        nc.gpsimd.memset(x_scales_sb[:].bitcast(I32), 0)
        nc.scalar.dma_start(gt_sb[:], gt.rearrange("(p t) o -> p (t o)", t=PACK))
        nc.sync.dma_start(wa_raw[0][:], wa_rows[:, :, half(0)])
        for q in range(4):
            nc.sync.dma_start(
                x_scales_sb[32 * q : 32 * q + 4, :].bitcast(I32), x_scales[0, 4 * q : 4 * q + 4, :].bitcast(I32)
            )
        nc.sync.dma_start(offs_sb[:], offs)
        nc.sync.dma_start(x_words_sb[:].bitcast(I32), x_words[0].rearrange("p n t -> p (n t)").bitcast(I32))
        nc.sync.dma_start(wa_raw[1][:], wa_rows[:, :, half(1)])
        nc.sync.dma_start(fl_sb[:], fl)
        nc.sync.dma_start(w1_raw[:], w1.rearrange("(p j) c -> p j c", j=PACK))
        nc.sync.dma_start(w2_raw[0][:], w2_rows[:, :, half(0)])
        nc.sync.dma_start(gp_sb, gp.rearrange("(p t) o -> p (t o)", t=PACK))
        nc.sync.dma_start(fm_sb[:], fm)
        nc.sync.dma_start(w2_raw[1][:], w2_rows[:, :, half(1)])
        nc.sync.dma_start(res_sb[:], res.rearrange("(t p) c -> p t c", p=P))

        picked_scales = sb("picked_scales", [P, S], U8)
        x_codes = sb("x_codes", [P, S], U32)
        x_plane = sb("x_plane", [P, S], U8)
        nc.vector.tensor_copy(picked_scales[:], x_scales_sb[:].indirect(offs_sb[:]))
        nc.vector.tensor_copy(
            x_plane[:].rearrange("p (t m) -> p t m", t=PACK), picked_scales[:].rearrange("p (m t) -> p t m", t=PACK)
        )
        nc.vector.tensor_copy(x_codes[:].rearrange("p (t m) -> p m t", t=PACK), x_words_sb[:].indirect(offs_sb[:]))
        x_packed = (x_codes, x_plane)

        wa_grouped = [sb("wa_grouped%d" % c, [P, PACK * HALF], BF16) for c in range(2)]
        wa_codes = sb("wa_codes", [P, H], U32)
        wa_plane = sb("wa_plane", [P, H], U8, "picked_scales")
        cut = WA_SCALAR_COLUMNS
        interleave(nc.scalar.copy, wa_grouped[0][:], wa_raw[0][:])
        interleave(nc.scalar.copy, wa_grouped[1][:, 0 : PACK * cut], wa_raw[1][:, :, 0:cut])
        interleave(nc.vector.tensor_copy, wa_grouped[1][:, PACK * cut : PACK * HALF], wa_raw[1][:, :, cut:HALF])
        for c in range(2):
            nc.vector.quantize_mx(
                out=wa_codes[:, half(c)].bitcast(FP8X4), scales=wa_plane[:, half(c)], in_=wa_grouped[c][:]
            )

        y_rows = [sb("y_rows%d" % t, [P, H], F32, "wa_raw1" if t == 0 else None) for t in range(PACK)]
        for c in range(2):
            acc = bank("y_first%d" % c, [P, HALF], (4, 0)[c])
            matmul(acc[:], x_packed, 0, (wa_codes[:, half(c)], wa_plane[:, half(c)]))
            nc.scalar.activation(y_rows[0][:, half(c)], acc[:], ACT.Copy, scale=gt_sb[:, 0:1])
        for t in range(1, PACK):
            acc = bank("y_acc%d" % t, [P, H], t)
            matmul(acc[:], x_packed, t, (wa_codes[:], wa_plane[:]))
            nc.scalar.activation(y_rows[t][:], acc[:], ACT.Copy, scale=gt_sb[:, t : t + 1])

        def fetch(planes, rows, lists, order):
            for t, c in order:
                picks = lists[:, c * HALF // LIST_ROWS : (c + 1) * HALF // LIST_ROWS]
                nc.vector.tensor_copy(planes[c][:, t * HALF : (t + 1) * HALF], rows[t][:].indirect(picks))

        def weave(name, copy, planes, tag=None):
            grouped = sb(name, [P, PACK * HALF], BF16, tag)
            interleave(copy, grouped[:], planes[:].rearrange("p (t c) -> p t c", t=PACK))
            return grouped

        def deal_w1(pair):
            grouped = sb("w1_grouped%d" % pair, [P, PACK * HALF], BF16)
            nc.scalar.copy(
                grouped[:].rearrange("p (t m j) -> p m j t", t=2, j=PACK),
                w1_raw[:].rearrange("p j (m t) -> p m j t", t=PACK)[:, :, :, 2 * pair : 2 * pair + 2],
            )
            return grouped

        def cast_w2(c, tag=None):
            grouped = sb("w2_grouped%d" % c, [P, PACK * HALF], BF16, tag)
            interleave(nc.scalar.copy, grouped[:], w2_raw[c][:])
            return grouped

        z_planes = [sb("z_planes%d" % c, [P, PACK * HALF], BF16, ("z_early", "z_late")[c]) for c in range(2)]
        fetch(z_planes, y_rows, fl_sb, [(t, c) for c in range(2) for t in range(PACK)])
        w1_packed = [quantize("w1_first", deal_w1(0))]
        z_packed = [quantize("z_first", weave("z_grouped0", nc.scalar.copy, z_planes[0]))]
        z_grouped = weave("z_grouped1", nc.vector.tensor_copy, z_planes[1], "z_early")
        w1_packed.append(quantize("w1_second", deal_w1(1)))
        z_packed.append(quantize("z_second", z_grouped))
        w2_grouped = cast_w2(0)

        h_rows = [sb("h_rows0", [P, H], F32, "z_late")] + y_rows[1:]
        h_relu = sb("h_relu", [P, 5 * HALF], F32, "w2_raw0")

        def h_product(acc, t, c):
            matmul(acc, w1_packed[t // 2], t % 2, (z_packed[c][0][:], z_packed[c][1][:]))

        def h_on_vector(t, c, number):
            acc = bank("h_acc%d_%d" % (t, c), [P, HALF], number)
            h_product(acc[:], t, c)
            nc.vector.tensor_scalar(h_rows[t][:, half(c)], acc[:], 0.0, gp_sb[:, t : t + 1], ALU.max, ALU.mult)

        def h_on_scalar(t, halves, number, staged):
            acc = bank("h_acc%d" % t, [P, len(halves) * HALF], number)
            for c in halves:
                h_product(acc[:, half(c)], t, c)
            nc.scalar.activation(staged, acc[:], ACT.Relu)
            nc.scalar.activation(h_rows[t][:, 0 : len(halves) * HALF], staged, ACT.Copy, scale=gp_sb[:, t : t + 1])

        h_on_vector(0, 0, 4)
        w2_packed = [quantize("w2_first", w2_grouped)]
        h_on_scalar(1, (0,), 5, h_relu[:, 0:HALF])
        h_on_vector(0, 1, 0)
        h_on_vector(1, 1, 1)
        h_on_scalar(2, (0, 1), 2, h_relu[:, HALF : 3 * HALF])
        h_on_scalar(3, (0, 1), 4, h_relu[:, 3 * HALF : 5 * HALF])

        fetch(z2_planes, h_rows, fm_sb, [(t, c) for pair in ((0, 1), (2, 3)) for c in range(2) for t in pair])
        w2_packed.append(quantize("w2_second", cast_w2(1, "w2_raw0")))
        z2_packed = [quantize("z2_first", weave("z2_grouped0", nc.scalar.copy, z2_planes[0]))]
        z2_packed.append(quantize("z2_second", weave("z2_grouped1", nc.vector.tensor_copy, z2_planes[1], "z2_early")))

        out_rows = out.rearrange("(t p) c -> p t c", p=P)
        groups = (((0, 2, 6), (2, 4, 7)), ((0, 2, 0), (2, 3, 1), (3, 4, 3)))
        for c in range(2):
            result = sb("result%d" % c, [P, PACK, HALF], F32, ("z2_late", None)[c])
            for first, last, number in groups[c]:
                acc = bank("out_acc%d_%d" % (c, first), [P, last - first, HALF], number)
                for t in range(first, last):
                    matmul(acc[:, t - first, :], w2_packed[t // 2], t % 2, (z2_packed[c][0][:], z2_packed[c][1][:]))
                nc.vector.tensor_tensor(result[:, first:last, :], acc[:], res_sb[:, first:last, half(c)], ALU.add)
                nc.sync.dma_start(out_rows[:, first:last, half(c)], result[:, first:last, :])
